import numpy as np
import ml_dtypes


def mxq(x, axis, fmt="e4m3"):
    dtype, down = {"e4m3": (ml_dtypes.float8_e4m3fn, 7), "e5m2": (ml_dtypes.float8_e5m2, 14)}[fmt]
    v = np.moveaxis(np.asarray(x, np.float32).astype(ml_dtypes.bfloat16).astype(np.float64), axis, -1)
    blocks = v.reshape(v.shape[:-1] + (-1, 32))
    amax = np.abs(blocks).max(-1, keepdims=True)
    byte = np.maximum(np.where(amax > 0, np.frexp(amax)[1] - 1 + 127, 0) - down, 1)
    scale = np.exp2(byte - 127.0)
    codes = (blocks / scale).astype(np.float32).astype(dtype).astype(np.float64)
    return np.moveaxis((codes * scale).reshape(v.shape), -1, axis)


WIDE = False


def mx_kscale(k):
    if not WIDE:
        return np.ones(k)
    levels = np.array([10, -10, 5, -5, 0])
    if k % 512:
        return np.exp2(np.random.permutation(np.resize(levels, k // 32))).repeat(32)
    a = np.empty((k // 512, 16))
    for p in range(k // 512):
        a[p, :8] = np.random.permutation(np.resize(levels, 8))
        for g in range(8):
            far = levels[np.abs(levels - a[p, g]) >= 10]
            a[p, g + 8] = far[np.random.randint(len(far))]
    return np.exp2(a.ravel()).repeat(32)


def f64(x):
    return np.asarray(x).astype(np.float64)


def striped(idx):
    return np.tile(np.asarray(idx).reshape(-1, 16).T, (8, 1)).astype(np.uint16)


def unstriped(offs):
    return offs[:16].T.reshape(-1).astype(np.int64)


E2M1 = np.array([0.0, 0.5, 1.0, 1.5, 2.0, 3.0, 4.0, 6.0, -0.0, -0.5, -1.0, -1.5, -2.0, -3.0, -4.0, -6.0])


def pack_weight(w, fmt):
    k, n = w.shape
    w = f64(np.asarray(w, np.float32).astype(ml_dtypes.bfloat16)).reshape(k // 32, 32, n)
    amax = np.abs(w).max(1)
    if fmt == "e4m3":
        byte = np.frexp(amax)[1] - 1 + 127 - 7
    else:
        mant, ex = np.frexp(amax / 6.0)
        byte = np.where(mant > 0.5, ex, ex - 1) + 127
    byte = np.clip(np.where(amax > 0, byte, 1), 1, 254)
    scaled = (w * np.exp2(127.0 - byte)[:, None, :]).reshape(k, n).astype(np.float32)
    by_word = np.ascontiguousarray(scaled.reshape(k // 512, 128, 4, n).transpose(0, 1, 3, 2))
    if fmt == "e4m3":
        words = by_word.astype(ml_dtypes.float8_e4m3fn).view(np.uint8)
    else:
        c = by_word.astype(ml_dtypes.float4_e2m1fn).view(np.uint8) & 0xF
        words = (c[..., 0::2] | (c[..., 1::2] << 4)).reshape(k // 512, 128, 2 * n)
    return np.ascontiguousarray(words), np.ascontiguousarray(byte.astype(np.uint8).reshape(k // 512, 16, n))


def unpack_weight(words, scales, fmt):
    g, _, n = scales.shape
    words = np.ascontiguousarray(words).reshape(g, 128, n, -1)
    if fmt == "e4m3":
        vals = words.view(ml_dtypes.float8_e4m3fn).astype(np.float64)
    else:
        nib = np.empty((g, 128, n, 4), np.uint8)
        nib[..., 0::2] = words & 0xF
        nib[..., 1::2] = words >> 4
        vals = E2M1[nib]
    vals = vals * np.repeat(np.exp2(scales.astype(np.float64) - 127.0), 8, axis=1)[..., None]
    return vals.transpose(0, 1, 3, 2).reshape(g * 512, n)


D, E, T, I, Q = 512, 512, 2048, 512, 128


def setup_inputs():
    n = np.random.standard_normal
    idx = np.random.permutation(T)[:I]
    fd = mx_kscale(D)
    fi = mx_kscale(I)
    ti = np.ones(T)
    ti[idx] = fi
    keysp = pack_weight(n((D, T)) / fd[:, None], "e2m1")
    return {
        "query": (n((D, Q)) * 0.7 / np.sqrt(D) * fd[:, None]).astype(np.float32),
        "query2": (n((D, Q)) * 0.7 / np.sqrt(D) * fd[:, None]).astype(np.float32),
        "keys_words": keysp[0],
        "keys_scales": keysp[1],
        "sharp": (np.random.uniform(0.3, 1.2, (Q, 1))).astype(np.float32),
        "os": (np.random.uniform(4.0, 16.0, (1, I)) * fi).astype(np.float32),
        "vals": (n((E, T)) / ti).astype(np.float32),
        "offs": striped(idx),
    }


def reference(query, query2, keys_words, keys_scales, sharp, os, vals, offs):
    idx = unstriped(offs)
    keysu = unpack_weight(keys_words, keys_scales, "e2m1")
    queryq = mxq(f64(query), 0, "e4m3")
    keysidxg = keysu[:, idx]
    a = queryq.T @ keysidxg
    query2q = mxq(f64(query2), 0, "e4m3")
    b = query2q.T @ keysidxg
    dl = a - b
    p = np.exp(a * 0.5) / (np.square(dl) * f64(sharp) + 1.0)
    z = np.sum(p, axis=1, keepdims=True)
    w = p / z
    wo1 = w * f64(os)
    wt1 = wo1.T
    vt1 = f64(vals)[:, idx].T
    wt1q = mxq(wt1, 0, "e4m3")
    vt1q = mxq(vt1, 0, "e4m3")
    o = wt1q.T @ vt1q
    return o

@@ -1,0 +1,191 @@
+from contextlib import ExitStack
+
+import concourse.mybir as mybir
+from concourse.masks import make_identity
+
+D, E, T, I, Q = 512, 512, 2048, 512, 128
+P = 128
+PACK = 4
+FLOPS = 2 * Q * I * D * 2 + 2 * Q * I * E
+
+F32 = mybir.dt.float32
+BF16 = mybir.dt.bfloat16
+I32 = mybir.dt.int32
+U32 = mybir.dt.uint32
+U16 = mybir.dt.uint16
+U8 = mybir.dt.uint8
+FP8X4 = mybir.dt.float8_e4m3fn_x4
+FP4X4 = mybir.dt.float4_e2m1fn_x4
+ALU = mybir.AluOpType
+ACT = mybir.ActivationFunctionType
+
+
+def tile_attend_alikescores_kernel(tc, query, query2, keys_words, keys_scales, sharp, slot_factor, vals, offs, out):
+    nc = tc.nc
+    blocks = E // P
+    with ExitStack() as ctx:
+        sb = ctx.enter_context(tc.tile_pool(name="sb", bufs=1))
+        ps = ctx.enter_context(tc.psum_pool(name="ps", bufs=1))
+        ps_turn = ctx.enter_context(tc.psum_pool(name="ps_turn", bufs=3))
+
+        offsets = sb.tile([P, I // 16], U16, name="offsets")
+        nc.sync.dma_start(offsets[:], offs)
+        key_pool = sb.tile([P, T], U16, name="key_pool")
+        nc.sync.dma_start(key_pool[:].bitcast(I32), keys_words[0].bitcast(I32))
+        scale_pool = sb.tile([P, T], U8, name="scale_pool")
+        nc.vector.memset(scale_pool[:].bitcast(I32), 0)
+        for quad in range(4):
+            nc.scalar.dma_start(
+                scale_pool[32 * quad : 32 * quad + 4, :].bitcast(I32),
+                keys_scales[0, 4 * quad : 4 * quad + 4, :].bitcast(I32),
+            )
+        q_raw = []
+        for n, src in enumerate((query, query2)):
+            raw = sb.tile([P, PACK, Q], F32, name=f"q_raw{n}")
+            nc.sync.dma_start(raw[:], src.rearrange("(p j) q -> p j q", j=PACK))
+            q_raw.append(raw)
+        val_pool = []
+        for j in range(blocks):
+            pool_j = sb.tile([P, T], F32, name=f"val_pool{j}", tag=f"val{j}", align_bytes=64)
+            nc.sync.dma_start(pool_j[:], vals[j * P : (j + 1) * P, :])
+            val_pool.append(pool_j)
+            if j == 0:
+                sharp_col = sb.tile([P, 1], F32, name="sharp_col")
+                nc.sync.dma_start(sharp_col[:], sharp)
+                os_cols = sb.tile([P, PACK], F32, name="os_cols")
+                nc.sync.dma_start(os_cols[:], slot_factor.rearrange("o (p t) -> (o p) t", t=PACK))
+
+        ident = sb.tile([P, P], F32, name="ident")
+        make_identity(nc, ident[:])
+        one = sb.tile([P, 1], F32, name="one")
+        nc.vector.memset(one[:], 1.0)
+        zero = sb.tile([P, 1], F32, name="zero")
+        nc.scalar.activation(zero[:], one[:], ACT.Ln)
+
+        key_codes = sb.tile([P, I], U16, name="key_codes", tag="keys", align_bytes=64)
+        nc.vector.tensor_copy(key_codes[:], key_pool[:].indirect(offsets[:]))
+        key_scales = sb.tile([P, I], U8, name="key_scales", align_bytes=64)
+        nc.vector.tensor_copy(key_scales[:], scale_pool[:].indirect(offsets[:]))
+
+        q_grouped = sb.tile([P, 2, Q, PACK], BF16, name="q_grouped", align_bytes=64)
+        for n in range(2):
+            nc.scalar.copy(
+                q_grouped[:, n, :, :].rearrange("p (c i) t -> p c t i", i=4),
+                q_raw[n][:].rearrange("p t (c i) -> p c t i", i=4),
+            )
+        q_codes = sb.tile([P, 2 * Q], U32, name="q_codes", align_bytes=64)
+        q_scales = sb.tile([P, 2 * Q], U8, name="q_scales", align_bytes=64)
+        nc.vector.quantize_mx(
+            out=q_codes[:].bitcast(FP8X4),
+            scales=q_scales[:],
+            in_=q_grouped[:].rearrange("p n q t -> p (n q t)"),
+        )
+        scores = []
+        for n in range(2):
+            bank = ps.tile([P, I], F32, name=f"score{n}")
+            nc.tensor.matmul_mx(
+                out=bank[:],
+                lhsT=q_codes[:, n * Q : (n + 1) * Q].bitcast(FP8X4),
+                lhsT_scale=q_scales[:, n * Q : (n + 1) * Q],
+                rhs=key_codes[:].bitcast(FP4X4),
+                rhs_scale=key_scales[:],
+                start=True,
+                stop=True,
+            )
+            scores.append(bank)
+
+        os_rows = ps.tile([P, PACK, P], F32, name="os_rows")
+        for t in range(PACK):
+            nc.tensor.transpose(os_rows[:, t, :], os_cols[:, t : t + 1].to_broadcast([P, P]), ident[:])
+
+        def turn(rows, grouped):
+            words = rows[:].bitcast(F32)
+            turned = ps_turn.tile([P, 2, P], F32, name="turned")
+            for u in range(2):
+                nc.tensor.transpose(turned[:, u, :], words[:, u : I // 2 : 2], ident[:])
+            nc.scalar.copy(grouped.bitcast(F32), turned[:].rearrange("p u r -> p r u"))
+
+        def gather_values(j, tag):
+            picked = sb.tile([P, I], BF16, name=f"picked{j}", tag=tag, align_bytes=64)
+            nc.vector.tensor_copy(picked[:], val_pool[j][:].indirect(offsets[:]))
+            return picked
+
+        neg_half_a = sb.tile([P, I], F32, name="neg_half_a")
+        neg_half_max = sb.tile([P, 1], F32, name="neg_half_max")
+        nc.vector.tensor_scalar(neg_half_a[:], scores[0][:], -0.5, None, ALU.mult, ALU.min, accum_out=neg_half_max[:])
+        half_diff = sb.tile([P, I], F32, name="half_diff")
+        nc.vector.scalar_tensor_tensor(half_diff[:], scores[1][:], 0.5, neg_half_a[:], ALU.mult, ALU.add)
+        diff_sq = sb.tile([P, I], F32, name="diff_sq", tag="sq")
+        nc.scalar.activation(diff_sq[:], half_diff[:], ACT.Square, bias=zero[:], scale=2.0)
+        log_div = sb.tile([P, I], F32, name="log_div")
+        nc.scalar.activation(log_div[:], diff_sq[:], ACT.Ln, bias=one[:], scale=sharp_col[:])
+        unit = sb.tile([P, 1], F32, name="unit", tag="sq")
+        nc.scalar.activation(unit[:], one[:], ACT.Exp, scale=0.0)
+        picked = [gather_values(0, "keys")]
+        logit = sb.tile([P, I], F32, name="logit", tag="val0", align_bytes=64)
+        nc.vector.scalar_tensor_tensor(logit[:], log_div[:], -1.0, neg_half_a[:], ALU.mult, ALU.subtract)
+        parts = sb.tile([P, I], F32, name="parts")
+        row_sum = sb.tile([P, 1], F32, name="row_sum")
+        nc.scalar.activation(parts[:], logit[:], ACT.Exp, bias=neg_half_max[:], scale=unit[:], accum_out=row_sum[:])
+        picked.append(gather_values(1, "picked1"))
+        picked.append(gather_values(2, "picked2"))
+        inv_sum = sb.tile([P, 1], F32, name="inv_sum", tag="val2", align_bytes=64)
+        nc.vector.reciprocal(inv_sum[:], row_sum[:])
+        weights = sb.tile([P, I], BF16, name="weights", align_bytes=64)
+        nc.vector.scalar_tensor_tensor(
+            weights[:].rearrange("q (p t) -> q p t", t=PACK),
+            parts[:].rearrange("q (p t) -> q p t", t=PACK),
+            inv_sum[:],
+            os_rows[:].rearrange("q t p -> q p t"),
+            ALU.mult,
+            ALU.mult,
+        )
+        picked.append(gather_values(3, "picked3"))
+
+        early = sb.tile([P, blocks, P, PACK], BF16, name="early", tag="val0", align_bytes=64)
+        for j in range(blocks - 1):
+            turn(picked[j], early[:, j, :, :])
+        turn(weights, early[:, blocks - 1, :, :])
+        late = sb.tile([P, P, PACK], BF16, name="late", align_bytes=64)
+        turn(picked[blocks - 1], late[:])
+
+        early_codes = sb.tile([P, blocks * P], U32, name="early_codes", tag="val3", align_bytes=64)
+        early_scales = sb.tile([P, blocks * P], U8, name="early_scales", align_bytes=64)
+        nc.vector.quantize_mx(
+            out=early_codes[:].bitcast(FP8X4),
+            scales=early_scales[:],
+            in_=early[:].rearrange("p j r t -> p (j r t)"),
+        )
+        late_codes = sb.tile([P, P], U32, name="late_codes", align_bytes=64)
+        late_scales = sb.tile([P, P], U8, name="late_scales", align_bytes=64)
+        nc.vector.quantize_mx(
+            out=late_codes[:].bitcast(FP8X4),
+            scales=late_scales[:],
+            in_=late[:].rearrange("p r t -> p (r t)"),
+        )
+
+        split = (blocks - 1) * P
+        w_cols = slice(split, split + Q)
+
+        def product(acc, v_codes, v_scales):
+            nc.tensor.matmul_mx(
+                out=acc,
+                lhsT=early_codes[:, w_cols].bitcast(FP8X4),
+                lhsT_scale=early_scales[:, w_cols],
+                rhs=v_codes.bitcast(FP8X4),
+                rhs_scale=v_scales,
+                start=True,
+                stop=True,
+            )
+
+        acc_early = ps.tile([P, split], F32, name="acc_early")
+        for cols in (slice(0, 2 * P), slice(2 * P, split)):
+            product(acc_early[:, cols], early_codes[:, cols], early_scales[:, cols])
+        res_early = sb.tile([P, split], F32, name="res_early")
+        nc.scalar.copy(res_early[:], acc_early[:])
+        nc.sync.dma_start(out[:, 0:split], res_early[:])
+        acc_late = ps.tile([P, P], F32, name="acc_late")
+        product(acc_late[:], late_codes[:], late_scales[:])
+        res_late = sb.tile([P, P], F32, name="res_late")
+        nc.vector.tensor_copy(res_late[:], acc_late[:])
+        nc.sync.dma_start(out[:, split:E], res_late[:])

@@ -1,11 +1,12 @@
 from contextlib import ExitStack
 
 import concourse.mybir as mybir
-from concourse.masks import make_identity
 
 D, E, T, I, Q = 512, 512, 2048, 512, 128
 P = 128
 PACK = 4
+POOL_BYTES = 4 * T
+HALF = I // 2
 FLOPS = 2 * Q * I * D * 2 + 2 * Q * I * E
 
 F32 = mybir.dt.float32
@@ -25,6 +26,7 @@ def tile_attend_alikescores_kernel(tc, query, query2, keys_words, keys_scales, s
     blocks = E // P
     with ExitStack() as ctx:
         sb = ctx.enter_context(tc.tile_pool(name="sb", bufs=1))
+        vb = ctx.enter_context(tc.tile_pool(name="vb", bufs=1))
         ps = ctx.enter_context(tc.psum_pool(name="ps", bufs=1))
         ps_turn = ctx.enter_context(tc.psum_pool(name="ps_turn", bufs=3))
 
@@ -44,30 +46,44 @@ def tile_attend_alikescores_kernel(tc, query, query2, keys_words, keys_scales, s
             raw = sb.tile([P, PACK, Q], F32, name=f"q_raw{n}")
             nc.sync.dma_start(raw[:], src.rearrange("(p j) q -> p j q", j=PACK))
             q_raw.append(raw)
+        blank = vb.tile([P, blocks * T], F32, name="blank", offset=0, align_bytes=64)
+        nc.gpsimd.memset(blank[:, 0:P], 0.0)
+        ident = sb.tile([P, P], F32, name="ident")
+        nc.gpsimd.affine_select(
+            out=ident[:],
+            in_=blank[:, 0:P],
+            compare_op=ALU.not_equal,
+            fill=1.0,
+            base=0,
+            pattern=[[-1, P]],
+            channel_multiplier=1,
+        )
         val_pool = []
         for j in range(blocks):
-            pool_j = sb.tile([P, T], F32, name=f"val_pool{j}", tag=f"val{j}", align_bytes=64)
+            pool_j = vb.tile([P, T], F32, name=f"val_pool{j}", offset=j * POOL_BYTES, align_bytes=64)
             nc.sync.dma_start(pool_j[:], vals[j * P : (j + 1) * P, :])
             val_pool.append(pool_j)
-            if j == 0:
-                sharp_col = sb.tile([P, 1], F32, name="sharp_col")
-                nc.sync.dma_start(sharp_col[:], sharp)
-                os_cols = sb.tile([P, PACK], F32, name="os_cols")
-                nc.sync.dma_start(os_cols[:], slot_factor.rearrange("o (p t) -> (o p) t", t=PACK))
+        sharp_col = sb.tile([P, 1], F32, name="sharp_col")
+        nc.gpsimd.dma_start(sharp_col[:], sharp)
+        os_cols = sb.tile([P, PACK], F32, name="os_cols")
+        nc.gpsimd.dma_start(os_cols[:], slot_factor.rearrange("o (p t) -> (o p) t", t=PACK))
 
-        ident = sb.tile([P, P], F32, name="ident")
-        make_identity(nc, ident[:])
         one = sb.tile([P, 1], F32, name="one")
         nc.vector.memset(one[:], 1.0)
         zero = sb.tile([P, 1], F32, name="zero")
         nc.scalar.activation(zero[:], one[:], ACT.Ln)
 
-        key_codes = sb.tile([P, I], U16, name="key_codes", tag="keys", align_bytes=64)
+        key_codes = sb.tile([P, I], U16, name="key_codes", align_bytes=64)
         nc.vector.tensor_copy(key_codes[:], key_pool[:].indirect(offsets[:]))
-        key_scales = sb.tile([P, I], U8, name="key_scales", align_bytes=64)
-        nc.vector.tensor_copy(key_scales[:], scale_pool[:].indirect(offsets[:]))
 
-        q_grouped = sb.tile([P, 2, Q, PACK], BF16, name="q_grouped", align_bytes=64)
+        def gather_key_scales(h, tag):
+            picked_scales = sb.tile([P, HALF], U8, name=f"key_scales{h}", tag=tag, align_bytes=64)
+            cols = slice(h * HALF // 16, (h + 1) * HALF // 16)
+            nc.vector.tensor_copy(picked_scales[:], scale_pool[:].indirect(offsets[:, cols]))
+            return picked_scales
+
+        key_scales = [gather_key_scales(0, "key_scales0")]
+        q_grouped = sb.tile([P, 2, Q, PACK], BF16, name="q_grouped", tag="q_grouped", align_bytes=64)
         for n in range(2):
             nc.scalar.copy(
                 q_grouped[:, n, :, :].rearrange("p (c i) t -> p c t i", i=4),
@@ -80,18 +96,20 @@ def tile_attend_alikescores_kernel(tc, query, query2, keys_words, keys_scales, s
             scales=q_scales[:],
             in_=q_grouped[:].rearrange("p n q t -> p (n q t)"),
         )
+        key_scales.append(gather_key_scales(1, "q_grouped"))
         scores = []
-        for n in range(2):
-            bank = ps.tile([P, I], F32, name=f"score{n}")
-            nc.tensor.matmul_mx(
-                out=bank[:],
-                lhsT=q_codes[:, n * Q : (n + 1) * Q].bitcast(FP8X4),
-                lhsT_scale=q_scales[:, n * Q : (n + 1) * Q],
-                rhs=key_codes[:].bitcast(FP4X4),
-                rhs_scale=key_scales[:],
-                start=True,
-                stop=True,
-            )
+        for h in range(2):
+            bank = ps.tile([P, 2, HALF], F32, name=f"scores{h}")
+            for n in range(2):
+                nc.tensor.matmul_mx(
+                    out=bank[:, n, :],
+                    lhsT=q_codes[:, n * Q : (n + 1) * Q].bitcast(FP8X4),
+                    lhsT_scale=q_scales[:, n * Q : (n + 1) * Q],
+                    rhs=key_codes[:, h * HALF : (h + 1) * HALF].bitcast(FP4X4),
+                    rhs_scale=key_scales[h][:],
+                    start=True,
+                    stop=True,
+                )
             scores.append(bank)
 
         os_rows = ps.tile([P, PACK, P], F32, name="os_rows")
@@ -111,25 +129,34 @@ def tile_attend_alikescores_kernel(tc, query, query2, keys_words, keys_scales, s
             return picked
 
         neg_half_a = sb.tile([P, I], F32, name="neg_half_a")
-        neg_half_max = sb.tile([P, 1], F32, name="neg_half_max")
-        nc.vector.tensor_scalar(neg_half_a[:], scores[0][:], -0.5, None, ALU.mult, ALU.min, accum_out=neg_half_max[:])
         half_diff = sb.tile([P, I], F32, name="half_diff")
-        nc.vector.scalar_tensor_tensor(half_diff[:], scores[1][:], 0.5, neg_half_a[:], ALU.mult, ALU.add)
         diff_sq = sb.tile([P, I], F32, name="diff_sq", tag="sq")
-        nc.scalar.activation(diff_sq[:], half_diff[:], ACT.Square, bias=zero[:], scale=2.0)
         log_div = sb.tile([P, I], F32, name="log_div")
-        nc.scalar.activation(log_div[:], diff_sq[:], ACT.Ln, bias=one[:], scale=sharp_col[:])
+        first_min = sb.tile([P, 1], F32, name="first_min", tag="first_min", align_bytes=64)
+        neg_half_max = sb.tile([P, 1], F32, name="neg_half_max")
+        halves = [slice(h * HALF, (h + 1) * HALF) for h in range(2)]
+        nc.vector.tensor_scalar(
+            neg_half_a[:, halves[0]], scores[0][:, 0, :], -0.5, None, ALU.mult, ALU.min, accum_out=first_min[:]
+        )
+        nc.vector.tensor_scalar(
+            neg_half_a[:, halves[1]], scores[1][:, 0, :], -0.5, first_min[:], ALU.mult, ALU.min, accum_out=neg_half_max[:]
+        )
+        for h in range(2):
+            cols = halves[h]
+            nc.vector.scalar_tensor_tensor(half_diff[:, cols], scores[h][:, 1, :], 0.5, neg_half_a[:, cols], ALU.mult, ALU.add)
+            nc.scalar.activation(diff_sq[:, cols], half_diff[:, cols], ACT.Square, bias=zero[:], scale=2.0)
+            nc.scalar.activation(log_div[:, cols], diff_sq[:, cols], ACT.Ln, bias=one[:], scale=sharp_col[:])
         unit = sb.tile([P, 1], F32, name="unit", tag="sq")
         nc.scalar.activation(unit[:], one[:], ACT.Exp, scale=0.0)
-        picked = [gather_values(0, "keys")]
-        logit = sb.tile([P, I], F32, name="logit", tag="val0", align_bytes=64)
+        picked = [gather_values(0, "first_min")]
+        logit = vb.tile([P, I], F32, name="logit", offset=0, align_bytes=64)
         nc.vector.scalar_tensor_tensor(logit[:], log_div[:], -1.0, neg_half_a[:], ALU.mult, ALU.subtract)
         parts = sb.tile([P, I], F32, name="parts")
         row_sum = sb.tile([P, 1], F32, name="row_sum")
         nc.scalar.activation(parts[:], logit[:], ACT.Exp, bias=neg_half_max[:], scale=unit[:], accum_out=row_sum[:])
         picked.append(gather_values(1, "picked1"))
         picked.append(gather_values(2, "picked2"))
-        inv_sum = sb.tile([P, 1], F32, name="inv_sum", tag="val2", align_bytes=64)
+        inv_sum = vb.tile([P, 1], F32, name="inv_sum", offset=2 * POOL_BYTES, align_bytes=64)
         nc.vector.reciprocal(inv_sum[:], row_sum[:])
         weights = sb.tile([P, I], BF16, name="weights", align_bytes=64)
         nc.vector.scalar_tensor_tensor(
@@ -142,14 +169,14 @@ def tile_attend_alikescores_kernel(tc, query, query2, keys_words, keys_scales, s
         )
         picked.append(gather_values(3, "picked3"))
 
-        early = sb.tile([P, blocks, P, PACK], BF16, name="early", tag="val0", align_bytes=64)
+        early = vb.tile([P, blocks, P, PACK], BF16, name="early", offset=0, align_bytes=64)
         for j in range(blocks - 1):
             turn(picked[j], early[:, j, :, :])
         turn(weights, early[:, blocks - 1, :, :])
         late = sb.tile([P, P, PACK], BF16, name="late", align_bytes=64)
         turn(picked[blocks - 1], late[:])
 
-        early_codes = sb.tile([P, blocks * P], U32, name="early_codes", tag="val3", align_bytes=64)
+        early_codes = vb.tile([P, blocks * P], U32, name="early_codes", offset=3 * POOL_BYTES, align_bytes=64)
         early_scales = sb.tile([P, blocks * P], U8, name="early_scales", align_bytes=64)
         nc.vector.quantize_mx(
             out=early_codes[:].bitcast(FP8X4),

@@ -84,10 +84,12 @@ def tile_attend_alikescores_kernel(tc, query, query2, keys_words, keys_scales, s
 
         key_scales = [gather_key_scales(0, "key_scales0")]
         q_grouped = sb.tile([P, 2, Q, PACK], BF16, name="q_grouped", tag="q_grouped", align_bytes=64)
-        for n in range(2):
-            nc.scalar.copy(
+        for n, sign in enumerate((1.0, -1.0)):
+            nc.scalar.activation(
                 q_grouped[:, n, :, :].rearrange("p (c i) t -> p c t i", i=4),
                 q_raw[n][:].rearrange("p t (c i) -> p c t i", i=4),
+                ACT.Copy,
+                scale=sign,
             )
         q_codes = sb.tile([P, 2 * Q], U32, name="q_codes", align_bytes=64)
         q_scales = sb.tile([P, 2 * Q], U8, name="q_scales", align_bytes=64)
@@ -97,20 +99,38 @@ def tile_attend_alikescores_kernel(tc, query, query2, keys_words, keys_scales, s
             in_=q_grouped[:].rearrange("p n q t -> p (n q t)"),
         )
         key_scales.append(gather_key_scales(1, "q_grouped"))
-        scores = []
-        for h in range(2):
-            bank = ps.tile([P, 2, HALF], F32, name=f"scores{h}")
-            for n in range(2):
-                nc.tensor.matmul_mx(
-                    out=bank[:, n, :],
-                    lhsT=q_codes[:, n * Q : (n + 1) * Q].bitcast(FP8X4),
-                    lhsT_scale=q_scales[:, n * Q : (n + 1) * Q],
-                    rhs=key_codes[:, h * HALF : (h + 1) * HALF].bitcast(FP4X4),
-                    rhs_scale=key_scales[h][:],
-                    start=True,
-                    stop=True,
-                )
-            scores.append(bank)
+
+        def score(dst, n, first, width, start, stop):
+            h = first // HALF
+            nc.tensor.matmul_mx(
+                out=dst,
+                lhsT=q_codes[:, n * Q : (n + 1) * Q].bitcast(FP8X4),
+                lhsT_scale=q_scales[:, n * Q : (n + 1) * Q],
+                rhs=key_codes[:, first : first + width].bitcast(FP4X4),
+                rhs_scale=key_scales[h][:, first - h * HALF : first - h * HALF + width],
+                start=start,
+                stop=stop,
+            )
+
+        def score_diff(dst, first):
+            score(dst, 0, first, P, True, False)
+            score(dst, 1, first, P, False, True)
+
+        a_bank = ps.tile([P, I], F32, name="a_bank")
+        neg_b = ps.tile([P, P], F32, name="neg_b", tag="neg_b")
+        diff1 = ps.tile([P, P], F32, name="diff1", tag="diff1")
+        diff23 = ps.tile([P, HALF], F32, name="diff23", tag="diff23")
+        a0 = sb.tile([P, P], F32, name="a0")
+        score(a_bank[:, 0:P], 0, 0, P, True, True)
+        score(neg_b[:], 1, 0, P, True, True)
+        nc.vector.tensor_copy(a0[:], a_bank[:, 0:P])
+        diff0 = sb.tile([P, P], F32, name="diff0")
+        nc.vector.tensor_tensor(diff0[:], neg_b[:], a0[:], ALU.add)
+        score_diff(diff1[:], P)
+        score_diff(diff23[:, 0:P], 2 * P)
+        score_diff(diff23[:, P:HALF], 3 * P)
+        score(a_bank[:, P:HALF], 0, P, P, True, True)
+        score(a_bank[:, HALF:I], 0, HALF, HALF, True, True)
 
         os_rows = ps.tile([P, PACK, P], F32, name="os_rows")
         for t in range(PACK):
@@ -128,29 +148,23 @@ def tile_attend_alikescores_kernel(tc, query, query2, keys_words, keys_scales, s
             nc.vector.tensor_copy(picked[:], val_pool[j][:].indirect(offsets[:]))
             return picked
 
-        neg_half_a = sb.tile([P, I], F32, name="neg_half_a")
-        half_diff = sb.tile([P, I], F32, name="half_diff")
         diff_sq = sb.tile([P, I], F32, name="diff_sq", tag="sq")
         log_div = sb.tile([P, I], F32, name="log_div")
-        first_min = sb.tile([P, 1], F32, name="first_min", tag="first_min", align_bytes=64)
-        neg_half_max = sb.tile([P, 1], F32, name="neg_half_max")
-        halves = [slice(h * HALF, (h + 1) * HALF) for h in range(2)]
-        nc.vector.tensor_scalar(
-            neg_half_a[:, halves[0]], scores[0][:, 0, :], -0.5, None, ALU.mult, ALU.min, accum_out=first_min[:]
-        )
-        nc.vector.tensor_scalar(
-            neg_half_a[:, halves[1]], scores[1][:, 0, :], -0.5, first_min[:], ALU.mult, ALU.min, accum_out=neg_half_max[:]
-        )
+        nc.scalar.activation(diff_sq[:, P:HALF], diff1[:], ACT.Square, bias=zero[:])
+        nc.scalar.activation(diff_sq[:, 0:P], diff0[:], ACT.Square, bias=zero[:])
+        nc.scalar.activation(diff_sq[:, HALF:I], diff23[:], ACT.Square, bias=zero[:])
         for h in range(2):
-            cols = halves[h]
-            nc.vector.scalar_tensor_tensor(half_diff[:, cols], scores[h][:, 1, :], 0.5, neg_half_a[:, cols], ALU.mult, ALU.add)
-            nc.scalar.activation(diff_sq[:, cols], half_diff[:, cols], ACT.Square, bias=zero[:], scale=2.0)
+            cols = slice(h * HALF, (h + 1) * HALF)
             nc.scalar.activation(log_div[:, cols], diff_sq[:, cols], ACT.Ln, bias=one[:], scale=sharp_col[:])
         unit = sb.tile([P, 1], F32, name="unit", tag="sq")
         nc.scalar.activation(unit[:], one[:], ACT.Exp, scale=0.0)
-        picked = [gather_values(0, "first_min")]
+        picked = [gather_values(0, "picked0")]
+        neg_max = vb.tile([P, 1], F32, name="neg_max", offset=4096, align_bytes=64)
+        nc.vector.tensor_reduce(neg_max[:], a_bank[:], mybir.AxisListType.X, ALU.max, negate=True)
         logit = vb.tile([P, I], F32, name="logit", offset=0, align_bytes=64)
-        nc.vector.scalar_tensor_tensor(logit[:], log_div[:], -1.0, neg_half_a[:], ALU.mult, ALU.subtract)
+        nc.vector.scalar_tensor_tensor(logit[:], a_bank[:], 0.5, log_div[:], ALU.mult, ALU.subtract)
+        neg_half_max = sb.tile([P, 1], F32, name="neg_half_max")
+        nc.vector.tensor_scalar(neg_half_max[:], neg_max[:], 0.5, None, ALU.mult)
         parts = sb.tile([P, I], F32, name="parts")
         row_sum = sb.tile([P, 1], F32, name="row_sum")
         nc.scalar.activation(parts[:], logit[:], ACT.Exp, bias=neg_half_max[:], scale=unit[:], accum_out=row_sum[:])
@@ -205,14 +219,16 @@ def tile_attend_alikescores_kernel(tc, query, query2, keys_words, keys_scales, s
                 stop=True,
             )
 
-        acc_early = ps.tile([P, split], F32, name="acc_early")
-        for cols in (slice(0, 2 * P), slice(2 * P, split)):
-            product(acc_early[:, cols], early_codes[:, cols], early_scales[:, cols])
-        res_early = sb.tile([P, split], F32, name="res_early")
-        nc.scalar.copy(res_early[:], acc_early[:])
-        nc.sync.dma_start(out[:, 0:split], res_early[:])
-        acc_late = ps.tile([P, P], F32, name="acc_late")
-        product(acc_late[:], late_codes[:], late_scales[:])
-        res_late = sb.tile([P, P], F32, name="res_late")
-        nc.vector.tensor_copy(res_late[:], acc_late[:])
-        nc.sync.dma_start(out[:, split:E], res_late[:])
+        acc01 = ps.tile([P, 2 * P], F32, name="acc01", tag="diff23")
+        product(acc01[:], early_codes[:, 0 : 2 * P], early_scales[:, 0 : 2 * P])
+        res01 = sb.tile([P, 2 * P], F32, name="res01")
+        nc.scalar.copy(res01[:], acc01[:])
+        nc.sync.dma_start(out[:, 0 : 2 * P], res01[:])
+        res23 = sb.tile([P, 2 * P], F32, name="res23")
+        acc2 = ps.tile([P, P], F32, name="acc2", tag="neg_b")
+        product(acc2[:], early_codes[:, 2 * P : split], early_scales[:, 2 * P : split])
+        acc3 = ps.tile([P, P], F32, name="acc3", tag="diff1")
+        product(acc3[:], late_codes[:], late_scales[:])
+        nc.vector.tensor_copy(res23[:, 0:P], acc2[:])
+        nc.vector.tensor_copy(res23[:, P : 2 * P], acc3[:])
+        nc.sync.dma_start(out[:, 2 * P : E], res23[:])

from contextlib import ExitStack

import concourse.mybir as mybir

D, E, T, I, Q = 512, 512, 2048, 512, 128
P = 128
PACK = 4
POOL_BYTES = 4 * T
HALF = I // 2
FLOPS = 2 * Q * I * D * 2 + 2 * Q * I * E

F32 = mybir.dt.float32
BF16 = mybir.dt.bfloat16
I32 = mybir.dt.int32
U32 = mybir.dt.uint32
U16 = mybir.dt.uint16
U8 = mybir.dt.uint8
FP8X4 = mybir.dt.float8_e4m3fn_x4
FP4X4 = mybir.dt.float4_e2m1fn_x4
ALU = mybir.AluOpType
ACT = mybir.ActivationFunctionType


def tile_attend_alikescores_kernel(tc, query, query2, keys_words, keys_scales, sharp, slot_factor, vals, offs, out):
    nc = tc.nc
    blocks = E // P
    with ExitStack() as ctx:
        sb = ctx.enter_context(tc.tile_pool(name="sb", bufs=1))
        vb = ctx.enter_context(tc.tile_pool(name="vb", bufs=1))
        ps = ctx.enter_context(tc.psum_pool(name="ps", bufs=1))
        ps_turn = ctx.enter_context(tc.psum_pool(name="ps_turn", bufs=3))

        offsets = sb.tile([P, I // 16], U16, name="offsets")
        nc.sync.dma_start(offsets[:], offs)
        key_pool = sb.tile([P, T], U16, name="key_pool")
        nc.sync.dma_start(key_pool[:].bitcast(I32), keys_words[0].bitcast(I32))
        scale_pool = sb.tile([P, T], U8, name="scale_pool")
        nc.vector.memset(scale_pool[:].bitcast(I32), 0)
        for quad in range(4):
            nc.scalar.dma_start(
                scale_pool[32 * quad : 32 * quad + 4, :].bitcast(I32),
                keys_scales[0, 4 * quad : 4 * quad + 4, :].bitcast(I32),
            )
        q_raw = []
        for n, src in enumerate((query, query2)):
            raw = sb.tile([P, PACK, Q], F32, name=f"q_raw{n}")
            nc.sync.dma_start(raw[:], src.rearrange("(p j) q -> p j q", j=PACK))
            q_raw.append(raw)
        blank = vb.tile([P, blocks * T], F32, name="blank", offset=0, align_bytes=64)
        nc.gpsimd.memset(blank[:, 0:P], 0.0)
        ident = sb.tile([P, P], F32, name="ident")
        nc.gpsimd.affine_select(
            out=ident[:],
            in_=blank[:, 0:P],
            compare_op=ALU.not_equal,
            fill=1.0,
            base=0,
            pattern=[[-1, P]],
            channel_multiplier=1,
        )
        val_pool = []
        for j in range(blocks):
            pool_j = vb.tile([P, T], F32, name=f"val_pool{j}", offset=j * POOL_BYTES, align_bytes=64)
            nc.sync.dma_start(pool_j[:], vals[j * P : (j + 1) * P, :])
            val_pool.append(pool_j)
        sharp_col = sb.tile([P, 1], F32, name="sharp_col")
        nc.gpsimd.dma_start(sharp_col[:], sharp)
        os_cols = sb.tile([P, PACK], F32, name="os_cols")
        nc.gpsimd.dma_start(os_cols[:], slot_factor.rearrange("o (p t) -> (o p) t", t=PACK))

        one = sb.tile([P, 1], F32, name="one")
        nc.vector.memset(one[:], 1.0)
        zero = sb.tile([P, 1], F32, name="zero")
        nc.scalar.activation(zero[:], one[:], ACT.Ln)

        key_codes = sb.tile([P, I], U16, name="key_codes", align_bytes=64)
        nc.vector.tensor_copy(key_codes[:], key_pool[:].indirect(offsets[:]))

        def gather_key_scales(h, tag):
            picked_scales = sb.tile([P, HALF], U8, name=f"key_scales{h}", tag=tag, align_bytes=64)
            cols = slice(h * HALF // 16, (h + 1) * HALF // 16)
            nc.vector.tensor_copy(picked_scales[:], scale_pool[:].indirect(offsets[:, cols]))
            return picked_scales

        key_scales = [gather_key_scales(0, "key_scales0")]
        q_grouped = sb.tile([P, 2, Q, PACK], BF16, name="q_grouped", tag="q_grouped", align_bytes=64)
        for n, sign in enumerate((1.0, -1.0)):
            nc.scalar.activation(
                q_grouped[:, n, :, :].rearrange("p (c i) t -> p c t i", i=4),
                q_raw[n][:].rearrange("p t (c i) -> p c t i", i=4),
                ACT.Copy,
                scale=sign,
            )
        q_codes = sb.tile([P, 2 * Q], U32, name="q_codes", align_bytes=64)
        q_scales = sb.tile([P, 2 * Q], U8, name="q_scales", align_bytes=64)
        nc.vector.quantize_mx(
            out=q_codes[:].bitcast(FP8X4),
            scales=q_scales[:],
            in_=q_grouped[:].rearrange("p n q t -> p (n q t)"),
        )
        key_scales.append(gather_key_scales(1, "q_grouped"))

        def score(dst, n, first, width, start, stop):
            h = first // HALF
            nc.tensor.matmul_mx(
                out=dst,
                lhsT=q_codes[:, n * Q : (n + 1) * Q].bitcast(FP8X4),
                lhsT_scale=q_scales[:, n * Q : (n + 1) * Q],
                rhs=key_codes[:, first : first + width].bitcast(FP4X4),
                rhs_scale=key_scales[h][:, first - h * HALF : first - h * HALF + width],
                start=start,
                stop=stop,
            )

        def score_diff(dst, first):
            score(dst, 0, first, P, True, False)
            score(dst, 1, first, P, False, True)

        a_bank = ps.tile([P, I], F32, name="a_bank")
        neg_b = ps.tile([P, P], F32, name="neg_b", tag="neg_b")
        diff1 = ps.tile([P, P], F32, name="diff1", tag="diff1")
        diff23 = ps.tile([P, HALF], F32, name="diff23", tag="diff23")
        a0 = sb.tile([P, P], F32, name="a0")
        score(a_bank[:, 0:P], 0, 0, P, True, True)
        score(neg_b[:], 1, 0, P, True, True)
        nc.vector.tensor_copy(a0[:], a_bank[:, 0:P])
        diff0 = sb.tile([P, P], F32, name="diff0")
        nc.vector.tensor_tensor(diff0[:], neg_b[:], a0[:], ALU.add)
        score_diff(diff1[:], P)
        score_diff(diff23[:, 0:P], 2 * P)
        score_diff(diff23[:, P:HALF], 3 * P)
        score(a_bank[:, P:HALF], 0, P, P, True, True)
        score(a_bank[:, HALF:I], 0, HALF, HALF, True, True)

        os_rows = ps.tile([P, PACK, P], F32, name="os_rows")
        for t in range(PACK):
            nc.tensor.transpose(os_rows[:, t, :], os_cols[:, t : t + 1].to_broadcast([P, P]), ident[:])

        def turn(rows, grouped):
            words = rows[:].bitcast(F32)
            turned = ps_turn.tile([P, 2, P], F32, name="turned")
            for u in range(2):
                nc.tensor.transpose(turned[:, u, :], words[:, u : I // 2 : 2], ident[:])
            nc.scalar.copy(grouped.bitcast(F32), turned[:].rearrange("p u r -> p r u"))

        def gather_values(j, tag):
            picked = sb.tile([P, I], BF16, name=f"picked{j}", tag=tag, align_bytes=64)
            nc.vector.tensor_copy(picked[:], val_pool[j][:].indirect(offsets[:]))
            return picked

        diff_sq = sb.tile([P, I], F32, name="diff_sq", tag="sq")
        log_div = sb.tile([P, I], F32, name="log_div")
        nc.scalar.activation(diff_sq[:, P:HALF], diff1[:], ACT.Square, bias=zero[:])
        nc.scalar.activation(diff_sq[:, 0:P], diff0[:], ACT.Square, bias=zero[:])
        nc.scalar.activation(diff_sq[:, HALF:I], diff23[:], ACT.Square, bias=zero[:])
        for h in range(2):
            cols = slice(h * HALF, (h + 1) * HALF)
            nc.scalar.activation(log_div[:, cols], diff_sq[:, cols], ACT.Ln, bias=one[:], scale=sharp_col[:])
        unit = sb.tile([P, 1], F32, name="unit", tag="sq")
        nc.scalar.activation(unit[:], one[:], ACT.Exp, scale=0.0)
        picked = [gather_values(0, "picked0")]
        neg_max = vb.tile([P, 1], F32, name="neg_max", offset=4096, align_bytes=64)
        nc.vector.tensor_reduce(neg_max[:], a_bank[:], mybir.AxisListType.X, ALU.max, negate=True)
        logit = vb.tile([P, I], F32, name="logit", offset=0, align_bytes=64)
        nc.vector.scalar_tensor_tensor(logit[:], a_bank[:], 0.5, log_div[:], ALU.mult, ALU.subtract)
        neg_half_max = sb.tile([P, 1], F32, name="neg_half_max")
        nc.vector.tensor_scalar(neg_half_max[:], neg_max[:], 0.5, None, ALU.mult)
        parts = sb.tile([P, I], F32, name="parts")
        row_sum = sb.tile([P, 1], F32, name="row_sum")
        nc.scalar.activation(parts[:], logit[:], ACT.Exp, bias=neg_half_max[:], scale=unit[:], accum_out=row_sum[:])
        picked.append(gather_values(1, "picked1"))
        picked.append(gather_values(2, "picked2"))
        inv_sum = vb.tile([P, 1], F32, name="inv_sum", offset=2 * POOL_BYTES, align_bytes=64)
        nc.vector.reciprocal(inv_sum[:], row_sum[:])
        weights = sb.tile([P, I], BF16, name="weights", align_bytes=64)
        nc.vector.scalar_tensor_tensor(
            weights[:].rearrange("q (p t) -> q p t", t=PACK),
            parts[:].rearrange("q (p t) -> q p t", t=PACK),
            inv_sum[:],
            os_rows[:].rearrange("q t p -> q p t"),
            ALU.mult,
            ALU.mult,
        )
        picked.append(gather_values(3, "picked3"))

        early = vb.tile([P, blocks, P, PACK], BF16, name="early", offset=0, align_bytes=64)
        for j in range(blocks - 1):
            turn(picked[j], early[:, j, :, :])
        turn(weights, early[:, blocks - 1, :, :])
        late = sb.tile([P, P, PACK], BF16, name="late", align_bytes=64)
        turn(picked[blocks - 1], late[:])

        early_codes = vb.tile([P, blocks * P], U32, name="early_codes", offset=3 * POOL_BYTES, align_bytes=64)
        early_scales = sb.tile([P, blocks * P], U8, name="early_scales", align_bytes=64)
        nc.vector.quantize_mx(
            out=early_codes[:].bitcast(FP8X4),
            scales=early_scales[:],
            in_=early[:].rearrange("p j r t -> p (j r t)"),
        )
        late_codes = sb.tile([P, P], U32, name="late_codes", align_bytes=64)
        late_scales = sb.tile([P, P], U8, name="late_scales", align_bytes=64)
        nc.vector.quantize_mx(
            out=late_codes[:].bitcast(FP8X4),
            scales=late_scales[:],
            in_=late[:].rearrange("p r t -> p (r t)"),
        )

        split = (blocks - 1) * P
        w_cols = slice(split, split + Q)

        def product(acc, v_codes, v_scales):
            nc.tensor.matmul_mx(
                out=acc,
                lhsT=early_codes[:, w_cols].bitcast(FP8X4),
                lhsT_scale=early_scales[:, w_cols],
                rhs=v_codes.bitcast(FP8X4),
                rhs_scale=v_scales,
                start=True,
                stop=True,
            )

        acc01 = ps.tile([P, 2 * P], F32, name="acc01", tag="diff23")
        product(acc01[:], early_codes[:, 0 : 2 * P], early_scales[:, 0 : 2 * P])
        res01 = sb.tile([P, 2 * P], F32, name="res01")
        nc.scalar.copy(res01[:], acc01[:])
        nc.sync.dma_start(out[:, 0 : 2 * P], res01[:])
        res23 = sb.tile([P, 2 * P], F32, name="res23")
        acc2 = ps.tile([P, P], F32, name="acc2", tag="neg_b")
        product(acc2[:], early_codes[:, 2 * P : split], early_scales[:, 2 * P : split])
        acc3 = ps.tile([P, P], F32, name="acc3", tag="diff1")
        product(acc3[:], late_codes[:], late_scales[:])
        nc.vector.tensor_copy(res23[:, 0:P], acc2[:])
        nc.vector.tensor_copy(res23[:, P : 2 * P], acc3[:])
        nc.sync.dma_start(out[:, 2 * P : E], res23[:])
